import numpy as np, ml_dtypes
CORES = [4,20,36,52,68,84,100,116,132,148,164,180,196,212,228,244]
N = 16
VB, TK = 1, 512
def setup_inputs(rng):
    h = (rng.standard_normal((128, TK), dtype=np.float32) / 8).astype(ml_dtypes.bfloat16)
    return {"h": np.broadcast_to(h, (N, 128, TK)).copy(), "w": rng.standard_normal((N, 128, VB * 128), dtype=np.float32).astype(ml_dtypes.bfloat16)}
def setup_inputs_big(rng):
    d = setup_inputs(rng)
    for k in ("h", "w"): d[k] = (d[k].astype(np.float32) * 1024.0).astype(d[k].dtype)
    return d
def setup_inputs_small(rng):
    d = setup_inputs(rng)
    for k in ("h", "w"): d[k] = (d[k].astype(np.float32) * (1 / 1024.0)).astype(d[k].dtype)
    return d
def setup_inputs_apart(rng):
    d = setup_inputs(rng)
    f = (10.0 ** rng.permutation(np.linspace(-1.5, 1.5, N))).astype(np.float32).reshape(N, 1, 1)
    for k in ("w",): d[k] = (d[k].astype(np.float32) * f).astype(d[k].dtype)
    return d
def setup_inputs_neg(rng):
    d = setup_inputs(rng)
    d["h"] = (np.abs(d["h"].astype(np.float32)) * 1048576.0).astype(d["h"].dtype); d["w"] = (-np.abs(d["w"].astype(np.float32))).astype(d["w"].dtype)
    return d
def reference(h, w):
    H, W = h.astype(np.float64), w.astype(np.float64)
    Z = np.concatenate([W[r].T @ H[r] for r in range(N)], axis=0)
    m = Z.max(axis=0)
    s = np.maximum(Z - 0.5 * m, 0.0).sum(axis=0)
    return {"m": np.broadcast_to(m.astype(np.float32), (N, 1, TK)), "s": np.broadcast_to(s.astype(np.float32), (N, 1, TK))}

@@ -1,0 +1,184 @@
+from concourse.bass import DstId, RemoteDMATransfer
+from concourse.mybir import AluOpType
+
+N, TK = 16, 512
+
+SCRATCH = {
+    "h_sb": ("sbuf", [128, 512], "bfloat16"),
+    "w_sb": ("sbuf", [128, 128], "bfloat16"),
+    "ps1": ("psum", [128, 512], "float32"),
+    "psT": ("psum", [128, 512], "float32"),
+    "psX": ("psum", [128, 512], "float32"),
+    "psS": ("psum", [128, 512], "float32"),
+    "a0": ("sbuf", [128, 128], "float32"),
+    "a1": ("sbuf", [128, 128], "float32"),
+    "t64": ("sbuf", [128, 64], "float32"),
+    "t32": ("sbuf", [128, 32], "float32"),
+    "t16": ("sbuf", [128, 16], "float32"),
+    "t8": ("sbuf", [128, 8], "float32"),
+    "lm": ("sbuf", [128, 4], "float32"),
+    "gm": ("sbuf", [128, 4], "float32"),
+    "c128": ("sbuf", [128, 4], "float32"),
+    "tot": ("sbuf", [128, 4], "float32"),
+    "sr": ("sbuf", [128, 4], "float32"),
+    "cb": ("sbuf", [128, 128], "float32"),
+    "kc": ("sbuf", [128, 8], "float32"),
+    "pat": ("sbuf", [16, 17], "float32"),
+    "patS": ("sbuf", [16, 16], "float32"),
+    "idr": ("dram", [17, 16], "float32"),
+    "seld": ("dram", [64, 4], "float32"),
+    "eye": ("sbuf", [16, 16], "float32"),
+    "sel": ("sbuf", [64, 4], "float32"),
+    "land1": ("dram", [16, 128, 4], "float32"),
+    "land2": ("dram", [16, 128, 4], "float32"),
+    "L1": ("sbuf", [16, 512], "float32"),
+    "L2": ("sbuf", [64, 128], "float32"),
+    "srow": ("sbuf", [4, 128], "float32"),
+}
+SEMAPHORES = ["v", "h", "w", "mm", "c1", "c2", "eye", "sel", "st1", "st2", "arr1", "arr2", "loc",
+              "l1", "l2", "t1", "t2", "mout", "sout"]
+
+
+def rank_program(g, core, T, topo):
+    rank = T.rank_of(core)
+    if rank is None:
+        return
+    S = T.sem
+    V, PE, SY, SC = g.vector, g.tensor, g.sync, g.scalar
+    MAX, ADD, SUB, MUL = AluOpType.max, AluOpType.add, AluOpType.subtract, AluOpType.mult
+    nv = [0]
+
+    def vwait():
+        if nv[0]:
+            V.wait_ge(S.v, nv[0])
+
+    def vdone(ins):
+        ins.then_inc(S.v, 1)
+        nv[0] += 1
+        return nv[0]
+
+    def tt(out, a, b, op):
+        vwait()
+        return vdone(V.tensor_tensor(out, a, b, op))
+
+    def cp(out, a):
+        vwait()
+        return vdone(V.tensor_copy(out, a))
+
+    def fill(ap, val):
+        vwait()
+        return vdone(V.memset(ap, val))
+
+    def halves(src, width, op, last):
+        bufs = {64: T.t64, 32: T.t32, 16: T.t16, 8: T.t8}
+        n = 0
+        while width > 4:
+            width //= 2
+            out = last if width == 4 else bufs[width]
+            n = tt(out[:, 0:width], src[:, 0:width], src[:, width:2 * width], op)
+            src = out
+        return n
+
+    peers = [c for c in T.cores if c != core]
+    common = topo.mask(core, peers[0])
+    for d in peers:
+        common &= topo.mask(core, d)
+    engines = [1 << b for b in range(16) if (common >> b) & 1]
+
+    def allgather(buf, sem):
+        trs = []
+        for e, eng in enumerate(engines):
+            mine = peers[e::len(engines)]
+            if not mine:
+                continue
+            ids = []
+            for d in mine:
+                rid, pid = topo.addr(d, core)
+                ids.append(DstId(rid=rid, pnc=pid))
+            trs.append(RemoteDMATransfer(dst_ids=ids, dma_engine_mask=eng, remote_sem=sem,
+                                         srcs=[buf[rank]], dsts=[buf[rank] for _ in mine]))
+        g.remote_dma_fused(trs, local_sem=S.loc)
+        return len(trs)
+
+    SY.dma_start(T.h_sb[:], T.h[:]).then_inc(S.h, 16)
+    SC.dma_start(T.w_sb[:], T.w[:]).then_inc(S.w, 16)
+
+    fill(T.pat[:], 0.0)
+    fill(T.pat[:, 0:1], 1.0)
+    fill(T.patS[:], 0.0)
+    for k in range(4):
+        n_pat = fill(T.patS[:, 5 * k:5 * k + 1], 1.0)
+    fill(T.kc[:, 0:4], 0.5)
+    fill(T.kc[:, 4:8], 64.0)
+    SC.wait_ge(S.v, n_pat)
+    SC.dma_start(T.idr[:], T.pat[:]).then_inc(S.c1, 16)
+    SC.dma_start(T.seld[:], T.patS[:]).then_inc(S.c2, 16)
+    SC.wait_ge(S.c1, 16)
+    SC.dma_start(T.eye[:], T.idr[0:16, :]).then_inc(S.eye, 16)
+    SC.wait_ge(S.c2, 16)
+    SC.dma_start(T.sel[:], T.seld[:]).then_inc(S.sel, 16)
+
+    PE.wait_ge(S.h, 16)
+    PE.wait_ge(S.w, 16)
+    for j in range(4):
+        PE.matmul(T.ps1[:, j::4], T.h_sb[:, j::4], T.w_sb[:], True, True).then_inc(S.mm, 1)
+
+    V.wait_ge(S.mm, 4)
+    cp(T.a0[:], T.ps1[:, 0:128])
+    tt(T.a1[:], T.ps1[:, 128:256], T.a0[:], MAX)
+    tt(T.a0[:], T.ps1[:, 256:384], T.a1[:], MAX)
+    tt(T.a1[:], T.ps1[:, 384:512], T.a0[:], MAX)
+    n_lm = halves(T.a1, 128, MAX, T.lm)
+
+    SY.wait_ge(S.v, n_lm)
+    SY.dma_start(T.land1[rank], T.lm[:]).then_inc(S.st1, 16)
+    g.wait_ge(S.st1, 16)
+    nloc = allgather(T.land1, S.arr1)
+    SY.wait_ge(S.st1, 16)
+    SY.wait_ge(S.arr1, len(peers))
+    SY.dma_start(T.L1[:], T.land1[:]).then_inc(S.l1, 16)
+    PE.wait_ge(S.l1, 16)
+    PE.wait_ge(S.eye, 16)
+    for j in range(4):
+        PE.matmul(T.psT[:, j:64:4], T.L1[:, j::4], T.eye[:], True, True).then_inc(S.t1, 1)
+    V.wait_ge(S.t1, 4)
+    cp(T.t64[:, 0:32], T.psT[:, 32:64])
+    tt(T.t32[:], T.psT[:, 0:32], T.t64[:, 0:32], MAX)
+    n_gm = halves(T.t32, 32, MAX, T.gm)
+    SC.wait_ge(S.v, n_gm)
+    SC.dma_start(T.m[:], T.gm[:]).then_inc(S.mout, 16)
+
+    tt(T.cb[:, 0:4], T.gm[:], T.kc[:, 0:4], MUL)
+    wd = 4
+    while wd < 128:
+        cp(T.cb[:, wd:2 * wd], T.cb[:, 0:wd])
+        wd *= 2
+    tt(T.a0[:], T.ps1[:, 0:128], T.cb[:], MAX)
+    tt(T.psX[:, 0:128], T.ps1[:, 128:256], T.cb[:], MAX)
+    tt(T.a1[:], T.psX[:, 0:128], T.a0[:], ADD)
+    tt(T.a0[:], T.ps1[:, 256:384], T.cb[:], MAX)
+    tt(T.psX[:, 128:256], T.ps1[:, 384:512], T.cb[:], MAX)
+    tt(T.psX[:, 256:384], T.psX[:, 128:256], T.a0[:], ADD)
+    tt(T.a0[:], T.psX[:, 256:384], T.a1[:], ADD)
+    halves(T.a0, 128, ADD, T.tot)
+    tt(T.c128[:], T.gm[:], T.kc[:, 4:8], MUL)
+    n_sr = tt(T.sr[:], T.tot[:], T.c128[:], SUB)
+
+    SY.wait_ge(S.v, n_sr)
+    SY.dma_start(T.land2[rank], T.sr[:]).then_inc(S.st2, 16)
+    g.wait_ge(S.st2, 16)
+    nloc += allgather(T.land2, S.arr2)
+    SY.wait_ge(S.st2, 16)
+    SY.wait_ge(S.arr2, len(peers))
+    SY.dma_start(T.L2[:], T.land2[:]).then_inc(S.l2, 16)
+    PE.wait_ge(S.l2, 16)
+    PE.wait_ge(S.sel, 16)
+    PE.matmul(T.psS[0:4, 0:128], T.sel[:], T.L2[:], True, True).then_inc(S.t2, 1)
+    V.wait_ge(S.t2, 1)
+    n_out = cp(T.srow[:], T.psS[0:4, 0:128])
+    SY.wait_ge(S.v, n_out)
+    SY.dma_start(T.s[:], T.srow[:]).then_inc(S.sout, 16)
+
+    g.wait_ge(S.loc, nloc)
+    SC.wait_ge(S.mout, 16)
+    SY.wait_ge(S.sout, 16)

@@ -6,28 +6,34 @@ N, TK = 16, 512
 SCRATCH = {
     "h_sb": ("sbuf", [128, 512], "bfloat16"),
     "w_sb": ("sbuf", [128, 128], "bfloat16"),
-    "ps1": ("psum", [128, 512], "float32"),
+    "psA": ("psum", [128, 512], "float32"),
+    "psB": ("psum", [128, 512], "float32"),
     "psT": ("psum", [128, 512], "float32"),
     "psX": ("psum", [128, 512], "float32"),
     "psS": ("psum", [128, 512], "float32"),
-    "a0": ("sbuf", [128, 128], "float32"),
-    "a1": ("sbuf", [128, 128], "float32"),
-    "t64": ("sbuf", [128, 64], "float32"),
-    "t32": ("sbuf", [128, 32], "float32"),
-    "t16": ("sbuf", [128, 16], "float32"),
-    "t8": ("sbuf", [128, 8], "float32"),
+    "p0": ("sbuf", [128, 128], "float32"),
+    "p1": ("sbuf", [128, 128], "float32"),
+    "p2": ("sbuf", [128, 128], "float32"),
+    "p3": ("sbuf", [128, 128], "float32"),
+    "x0": ("sbuf", [128, 128], "float32"),
+    "x2": ("sbuf", [128, 128], "float32"),
+    "y0": ("sbuf", [128, 128], "float32"),
+    "y": ("sbuf", [128, 128], "float32"),
+    "ta": ("sbuf", [128, 128], "float32"),
+    "tb": ("sbuf", [128, 128], "float32"),
+    "tc": ("sbuf", [128, 128], "float32"),
+    "u64": ("sbuf", [128, 64], "float32"),
     "lm": ("sbuf", [128, 4], "float32"),
-    "gm": ("sbuf", [128, 4], "float32"),
+    "mc": ("sbuf", [128, 132], "float32"),
     "c128": ("sbuf", [128, 4], "float32"),
     "tot": ("sbuf", [128, 4], "float32"),
     "sr": ("sbuf", [128, 4], "float32"),
-    "cb": ("sbuf", [128, 128], "float32"),
-    "kc": ("sbuf", [128, 8], "float32"),
-    "pat": ("sbuf", [16, 17], "float32"),
+    "kc": ("sbuf", [128, 4], "float32"),
+    "pat": ("sbuf", [16, 34], "float32"),
     "patS": ("sbuf", [16, 16], "float32"),
-    "idr": ("dram", [17, 16], "float32"),
+    "idr": ("dram", [17, 32], "float32"),
     "seld": ("dram", [64, 4], "float32"),
-    "eye": ("sbuf", [16, 16], "float32"),
+    "eye": ("sbuf", [16, 32], "float32"),
     "sel": ("sbuf", [64, 4], "float32"),
     "land1": ("dram", [16, 128, 4], "float32"),
     "land2": ("dram", [16, 128, 4], "float32"),
@@ -35,7 +41,7 @@ SCRATCH = {
     "L2": ("sbuf", [64, 128], "float32"),
     "srow": ("sbuf", [4, 128], "float32"),
 }
-SEMAPHORES = ["v", "h", "w", "mm", "c1", "c2", "eye", "sel", "st1", "st2", "arr1", "arr2", "loc",
+SEMAPHORES = ["v", "h", "w", "mma", "mmb", "c1", "c2", "eye", "sel", "st1", "st2", "arr1", "arr2", "loc",
               "l1", "l2", "t1", "t2", "mout", "sout"]
 
 
@@ -48,35 +54,32 @@ def rank_program(g, core, T, topo):
     MAX, ADD, SUB, MUL = AluOpType.max, AluOpType.add, AluOpType.subtract, AluOpType.mult
     nv = [0]
 
-    def vwait():
+    def sync():
         if nv[0]:
             V.wait_ge(S.v, nv[0])
 
-    def vdone(ins):
+    def done(ins):
         ins.then_inc(S.v, 1)
         nv[0] += 1
         return nv[0]
 
     def tt(out, a, b, op):
-        vwait()
-        return vdone(V.tensor_tensor(out, a, b, op))
+        return done(V.tensor_tensor(out, a, b, op))
 
     def cp(out, a):
-        vwait()
-        return vdone(V.tensor_copy(out, a))
+        return done(V.tensor_copy(out, a))
 
     def fill(ap, val):
-        vwait()
-        return vdone(V.memset(ap, val))
+        return done(V.memset(ap, val))
 
-    def halves(src, width, op, last):
-        bufs = {64: T.t64, 32: T.t32, 16: T.t16, 8: T.t8}
-        n = 0
-        while width > 4:
+    def halves(src, base, width, op, lv, last, lbase, stop=4):
+        n, off = 0, 0
+        while width > stop:
             width //= 2
-            out = last if width == 4 else bufs[width]
-            n = tt(out[:, 0:width], src[:, 0:width], src[:, width:2 * width], op)
-            src = out
+            dst, dbase = (last, lbase) if width == stop else (lv, off)
+            sync()
+            n = tt(dst[:, dbase:dbase + width], src[:, base:base + width], src[:, base + width:base + 2 * width], op)
+            src, base, off = dst, dbase, off + width
         return n
 
     peers = [c for c in T.cores if c != core]
@@ -103,14 +106,16 @@ def rank_program(g, core, T, topo):
     SY.dma_start(T.h_sb[:], T.h[:]).then_inc(S.h, 16)
     SC.dma_start(T.w_sb[:], T.w[:]).then_inc(S.w, 16)
 
-    fill(T.pat[:], 0.0)
     fill(T.pat[:, 0:1], 1.0)
+    fill(T.pat[:, 1:2], 0.5)
+    fill(T.pat[:, 2:34], 0.0)
+    fill(T.kc[:], 64.0)
     fill(T.patS[:], 0.0)
+    sync()
     for k in range(4):
         n_pat = fill(T.patS[:, 5 * k:5 * k + 1], 1.0)
-    fill(T.kc[:, 0:4], 0.5)
-    fill(T.kc[:, 4:8], 64.0)
     SC.wait_ge(S.v, n_pat)
+    SC.wait_ge(S.h, 16)
     SC.dma_start(T.idr[:], T.pat[:]).then_inc(S.c1, 16)
     SC.dma_start(T.seld[:], T.patS[:]).then_inc(S.c2, 16)
     SC.wait_ge(S.c1, 16)
@@ -121,14 +126,22 @@ def rank_program(g, core, T, topo):
     PE.wait_ge(S.h, 16)
     PE.wait_ge(S.w, 16)
     for j in range(4):
-        PE.matmul(T.ps1[:, j::4], T.h_sb[:, j::4], T.w_sb[:], True, True).then_inc(S.mm, 1)
+        PE.matmul(T.psA[:, j:256:4], T.h_sb[:, j::4], T.w_sb[:, 0:64], True, True).then_inc(S.mma, 1)
+    for j in range(4):
+        PE.matmul(T.psB[:, j:256:4], T.h_sb[:, j::4], T.w_sb[:, 64:128], True, True).then_inc(S.mmb, 1)
+    z = [T.psA[:, 0:128], T.psA[:, 128:256], T.psB[:, 0:128], T.psB[:, 128:256]]
 
-    V.wait_ge(S.mm, 4)
-    cp(T.a0[:], T.ps1[:, 0:128])
-    tt(T.a1[:], T.ps1[:, 128:256], T.a0[:], MAX)
-    tt(T.a0[:], T.ps1[:, 256:384], T.a1[:], MAX)
-    tt(T.a1[:], T.ps1[:, 384:512], T.a0[:], MAX)
-    n_lm = halves(T.a1, 128, MAX, T.lm)
+    sync()
+    V.wait_ge(S.mma, 4)
+    cp(T.p0[:], z[0])
+    sync()
+    tt(T.p1[:], z[1], T.p0[:], MAX)
+    sync()
+    V.wait_ge(S.mmb, 4)
+    tt(T.p2[:], z[2], T.p1[:], MAX)
+    sync()
+    tt(T.p3[:], z[3], T.p2[:], MAX)
+    n_lm = halves(T.p3, 0, 128, MAX, T.ta, T.lm, 0)
 
     SY.wait_ge(S.v, n_lm)
     SY.dma_start(T.land1[rank], T.lm[:]).then_inc(S.st1, 16)
@@ -140,28 +153,35 @@ def rank_program(g, core, T, topo):
     PE.wait_ge(S.l1, 16)
     PE.wait_ge(S.eye, 16)
     for j in range(4):
-        PE.matmul(T.psT[:, j:64:4], T.L1[:, j::4], T.eye[:], True, True).then_inc(S.t1, 1)
+        PE.matmul(T.psT[:, j:128:4], T.L1[:, j::4], T.eye[:], True, True).then_inc(S.t1, 1)
+    sync()
     V.wait_ge(S.t1, 4)
-    cp(T.t64[:, 0:32], T.psT[:, 32:64])
-    tt(T.t32[:], T.psT[:, 0:32], T.t64[:, 0:32], MAX)
-    n_gm = halves(T.t32, 32, MAX, T.gm)
+    cp(T.u64[:], T.psT[:, 64:128])
+    sync()
+    tt(T.tb[:, 64:128], T.psT[:, 0:64], T.u64[:], MAX)
+    n_gm = halves(T.tb, 64, 64, MAX, T.tb, T.mc, 0, stop=8)
     SC.wait_ge(S.v, n_gm)
-    SC.dma_start(T.m[:], T.gm[:]).then_inc(S.mout, 16)
+    SC.dma_start(T.m[:], T.mc[:, 0:4]).then_inc(S.mout, 16)
 
-    tt(T.cb[:, 0:4], T.gm[:], T.kc[:, 0:4], MUL)
+    sync()
+    tt(T.c128[:], T.mc[:, 0:4], T.kc[:], MUL)
     wd = 4
     while wd < 128:
-        cp(T.cb[:, wd:2 * wd], T.cb[:, 0:wd])
+        cp(T.mc[:, 4 + wd:4 + 2 * wd], T.mc[:, 4:4 + wd])
+        sync()
         wd *= 2
-    tt(T.a0[:], T.ps1[:, 0:128], T.cb[:], MAX)
-    tt(T.psX[:, 0:128], T.ps1[:, 128:256], T.cb[:], MAX)
-    tt(T.a1[:], T.psX[:, 0:128], T.a0[:], ADD)
-    tt(T.a0[:], T.ps1[:, 256:384], T.cb[:], MAX)
-    tt(T.psX[:, 128:256], T.ps1[:, 384:512], T.cb[:], MAX)
-    tt(T.psX[:, 256:384], T.psX[:, 128:256], T.a0[:], ADD)
-    tt(T.a0[:], T.psX[:, 256:384], T.a1[:], ADD)
-    halves(T.a0, 128, ADD, T.tot)
-    tt(T.c128[:], T.gm[:], T.kc[:, 4:8], MUL)
+    cb = T.mc[:, 4:132]
+    tt(T.x0[:], z[0], cb, MAX)
+    tt(T.psX[:, 0:128], z[1], cb, MAX)
+    tt(T.x2[:], z[2], cb, MAX)
+    tt(T.psX[:, 128:256], z[3], cb, MAX)
+    sync()
+    tt(T.y0[:], T.psX[:, 0:128], T.x0[:], ADD)
+    tt(T.psX[:, 256:384], T.psX[:, 128:256], T.x2[:], ADD)
+    sync()
+    tt(T.y[:], T.psX[:, 256:384], T.y0[:], ADD)
+    halves(T.y, 0, 128, ADD, T.tc, T.tot, 0)
+    sync()
     n_sr = tt(T.sr[:], T.tot[:], T.c128[:], SUB)
 
     SY.wait_ge(S.v, n_sr)
@@ -174,6 +194,7 @@ def rank_program(g, core, T, topo):
     PE.wait_ge(S.l2, 16)
     PE.wait_ge(S.sel, 16)
     PE.matmul(T.psS[0:4, 0:128], T.sel[:], T.L2[:], True, True).then_inc(S.t2, 1)
+    sync()
     V.wait_ge(S.t2, 1)
     n_out = cp(T.srow[:], T.psS[0:4, 0:128])
     SY.wait_ge(S.v, n_out)

@@ -2,6 +2,7 @@ from concourse.bass import DstId, RemoteDMATransfer
 from concourse.mybir import AluOpType
 
 N, TK = 16, 512
+NOPS = 64
 
 SCRATCH = {
     "h_sb": ("sbuf", [128, 512], "bfloat16"),
@@ -10,21 +11,16 @@ SCRATCH = {
     "psB": ("psum", [128, 512], "float32"),
     "psT": ("psum", [128, 512], "float32"),
     "psX": ("psum", [128, 512], "float32"),
+    "psY": ("psum", [128, 512], "float32"),
     "psS": ("psum", [128, 512], "float32"),
-    "p0": ("sbuf", [128, 128], "float32"),
-    "p1": ("sbuf", [128, 128], "float32"),
-    "p2": ("sbuf", [128, 128], "float32"),
-    "p3": ("sbuf", [128, 128], "float32"),
-    "x0": ("sbuf", [128, 128], "float32"),
-    "x2": ("sbuf", [128, 128], "float32"),
-    "y0": ("sbuf", [128, 128], "float32"),
-    "y": ("sbuf", [128, 128], "float32"),
+    "sa": ("sbuf", [128, 512], "float32"),
+    "sb": ("sbuf", [128, 512], "float32"),
     "ta": ("sbuf", [128, 128], "float32"),
     "tb": ("sbuf", [128, 128], "float32"),
     "tc": ("sbuf", [128, 128], "float32"),
     "u64": ("sbuf", [128, 64], "float32"),
     "lm": ("sbuf", [128, 4], "float32"),
-    "mc": ("sbuf", [128, 132], "float32"),
+    "mc": ("sbuf", [128, 68], "float32"),
     "c128": ("sbuf", [128, 4], "float32"),
     "tot": ("sbuf", [128, 4], "float32"),
     "sr": ("sbuf", [128, 4], "float32"),
@@ -41,8 +37,8 @@ SCRATCH = {
     "L2": ("sbuf", [64, 128], "float32"),
     "srow": ("sbuf", [4, 128], "float32"),
 }
-SEMAPHORES = ["v", "h", "w", "mma", "mmb", "c1", "c2", "eye", "sel", "st1", "st2", "arr1", "arr2", "loc",
-              "l1", "l2", "t1", "t2", "mout", "sout"]
+SEMAPHORES = ["h", "w", "mma", "mmb", "c1", "c2", "eye", "sel", "st1", "st2", "arr1", "arr2", "loc",
+              "l1", "l2", "t1", "t2", "mout", "sout"] + ["d%d" % i for i in range(NOPS)]
 
 
 def rank_program(g, core, T, topo):
@@ -52,35 +48,51 @@ def rank_program(g, core, T, topo):
     S = T.sem
     V, PE, SY, SC = g.vector, g.tensor, g.sync, g.scalar
     MAX, ADD, SUB, MUL = AluOpType.max, AluOpType.add, AluOpType.subtract, AluOpType.mult
-    nv = [0]
+    anc = []
+    seen = set()
 
-    def sync():
-        if nv[0]:
-            V.wait_ge(S.v, nv[0])
+    def dsem(k):
+        return S["d%d" % k]
 
-    def done(ins):
-        ins.then_inc(S.v, 1)
-        nv[0] += 1
-        return nv[0]
+    def need(deps):
+        for d in deps:
+            if d not in seen:
+                V.wait_ge(dsem(d), 1)
+                seen.add(d)
+                seen.update(anc[d])
 
-    def tt(out, a, b, op):
-        return done(V.tensor_tensor(out, a, b, op))
+    def done(ins, deps):
+        k = len(anc)
+        ins.then_inc(dsem(k), 1)
+        a = set(deps)
+        for d in deps:
+            a.update(anc[d])
+        anc.append(a)
+        return k
 
-    def cp(out, a):
-        return done(V.tensor_copy(out, a))
+    def tt(out, a, b, op, deps):
+        need(deps)
+        return done(V.tensor_tensor(out, a, b, op), deps)
 
-    def fill(ap, val):
-        return done(V.memset(ap, val))
+    def cp(out, a, deps):
+        need(deps)
+        return done(V.tensor_copy(out, a), deps)
 
-    def halves(src, base, width, op, lv, last, lbase, stop=4):
-        n, off = 0, 0
+    def fill(ap, val, deps=()):
+        need(deps)
+        return done(V.memset(ap, val), deps)
+
+    def halves(src, base, width, op, lv, last, lbase, dep, stop=4):
+        off = 0
         while width > stop:
             width //= 2
             dst, dbase = (last, lbase) if width == stop else (lv, off)
-            sync()
-            n = tt(dst[:, dbase:dbase + width], src[:, base:base + width], src[:, base + width:base + 2 * width], op)
+            dep = tt(dst[:, dbase:dbase + width], src[:, base:base + width], src[:, base + width:base + 2 * width], op, [dep])
             src, base, off = dst, dbase, off + width
-        return n
+        return dep
+
+    def blk(buf, i):
+        return buf[:, 64 * i:64 * i + 64]
 
     peers = [c for c in T.cores if c != core]
     common = topo.mask(core, peers[0])
@@ -106,15 +118,12 @@ def rank_program(g, core, T, topo):
     SY.dma_start(T.h_sb[:], T.h[:]).then_inc(S.h, 16)
     SC.dma_start(T.w_sb[:], T.w[:]).then_inc(S.w, 16)
 
-    fill(T.pat[:, 0:1], 1.0)
-    fill(T.pat[:, 1:2], 0.5)
-    fill(T.pat[:, 2:34], 0.0)
-    fill(T.kc[:], 64.0)
-    fill(T.patS[:], 0.0)
-    sync()
-    for k in range(4):
-        n_pat = fill(T.patS[:, 5 * k:5 * k + 1], 1.0)
-    SC.wait_ge(S.v, n_pat)
+    fp = [fill(T.pat[:, 0:1], 1.0), fill(T.pat[:, 1:2], 0.5), fill(T.pat[:, 2:34], 0.0)]
+    f_kc = fill(T.kc[:], 64.0)
+    f0 = fill(T.patS[:], 0.0)
+    fs = [fill(T.patS[:, 5 * k:5 * k + 1], 1.0, [f0]) for k in range(4)]
+    for k in fp + fs:
+        SC.wait_ge(dsem(k), 1)
     SC.wait_ge(S.h, 16)
     SC.dma_start(T.idr[:], T.pat[:]).then_inc(S.c1, 16)
     SC.dma_start(T.seld[:], T.patS[:]).then_inc(S.c2, 16)
@@ -129,21 +138,18 @@ def rank_program(g, core, T, topo):
         PE.matmul(T.psA[:, j:256:4], T.h_sb[:, j::4], T.w_sb[:, 0:64], True, True).then_inc(S.mma, 1)
     for j in range(4):
         PE.matmul(T.psB[:, j:256:4], T.h_sb[:, j::4], T.w_sb[:, 64:128], True, True).then_inc(S.mmb, 1)
-    z = [T.psA[:, 0:128], T.psA[:, 128:256], T.psB[:, 0:128], T.psB[:, 128:256]]
 
-    sync()
     V.wait_ge(S.mma, 4)
-    cp(T.p0[:], z[0])
-    sync()
-    tt(T.p1[:], z[1], T.p0[:], MAX)
-    sync()
+    c = [cp(blk(T.sa, i), blk(T.psA, i), []) for i in range(4)]
     V.wait_ge(S.mmb, 4)
-    tt(T.p2[:], z[2], T.p1[:], MAX)
-    sync()
-    tt(T.p3[:], z[3], T.p2[:], MAX)
-    n_lm = halves(T.p3, 0, 128, MAX, T.ta, T.lm, 0)
+    l1 = [tt(blk(T.psX, i // 2) if i % 2 else blk(T.sa, 4 + i // 2), blk(T.psB, i), blk(T.sa, i), MAX, [c[i]])
+          for i in range(4)]
+    l2a = tt(blk(T.sa, 6), blk(T.psX, 0), blk(T.sa, 4), MAX, [l1[0], l1[1]])
+    l2b = tt(blk(T.psX, 2), blk(T.psX, 1), blk(T.sa, 5), MAX, [l1[2], l1[3]])
+    l3 = tt(blk(T.sa, 7), blk(T.psX, 2), blk(T.sa, 6), MAX, [l2a, l2b])
+    k_lm = halves(T.sa, 448, 64, MAX, T.ta, T.lm, 0, l3)
 
-    SY.wait_ge(S.v, n_lm)
+    SY.wait_ge(dsem(k_lm), 1)
     SY.dma_start(T.land1[rank], T.lm[:]).then_inc(S.st1, 16)
     g.wait_ge(S.st1, 16)
     nloc = allgather(T.land1, S.arr1)
@@ -154,37 +160,29 @@ def rank_program(g, core, T, topo):
     PE.wait_ge(S.eye, 16)
     for j in range(4):
         PE.matmul(T.psT[:, j:128:4], T.L1[:, j::4], T.eye[:], True, True).then_inc(S.t1, 1)
-    sync()
     V.wait_ge(S.t1, 4)
-    cp(T.u64[:], T.psT[:, 64:128])
-    sync()
-    tt(T.tb[:, 64:128], T.psT[:, 0:64], T.u64[:], MAX)
-    n_gm = halves(T.tb, 64, 64, MAX, T.tb, T.mc, 0, stop=8)
-    SC.wait_ge(S.v, n_gm)
+    k = cp(T.u64[:], T.psT[:, 64:128], [])
+    k = tt(T.tb[:, 64:128], T.psT[:, 0:64], T.u64[:], MAX, [k])
+    k_gm = halves(T.tb, 64, 64, MAX, T.tb, T.mc, 0, k, stop=8)
+    SC.wait_ge(dsem(k_gm), 1)
     SC.dma_start(T.m[:], T.mc[:, 0:4]).then_inc(S.mout, 16)
 
-    sync()
-    tt(T.c128[:], T.mc[:, 0:4], T.kc[:], MUL)
-    wd = 4
-    while wd < 128:
-        cp(T.mc[:, 4 + wd:4 + 2 * wd], T.mc[:, 4:4 + wd])
-        sync()
-        wd *= 2
-    cb = T.mc[:, 4:132]
-    tt(T.x0[:], z[0], cb, MAX)
-    tt(T.psX[:, 0:128], z[1], cb, MAX)
-    tt(T.x2[:], z[2], cb, MAX)
-    tt(T.psX[:, 128:256], z[3], cb, MAX)
-    sync()
-    tt(T.y0[:], T.psX[:, 0:128], T.x0[:], ADD)
-    tt(T.psX[:, 256:384], T.psX[:, 128:256], T.x2[:], ADD)
-    sync()
-    tt(T.y[:], T.psX[:, 256:384], T.y0[:], ADD)
-    halves(T.y, 0, 128, ADD, T.tc, T.tot, 0)
-    sync()
-    n_sr = tt(T.sr[:], T.tot[:], T.c128[:], SUB)
+    b1 = [cp(T.mc[:, 4 + 4 * i:8 + 4 * i], T.mc[:, 4:8], [k_gm]) for i in range(1, 4)]
+    k_c128 = tt(T.c128[:], T.mc[:, 0:4], T.kc[:], MUL, [k_gm, f_kc])
+    b2 = [cp(T.mc[:, 4 + 16 * i:20 + 16 * i], T.mc[:, 4:20], b1) for i in range(1, 4)]
+    cb = T.mc[:, 4:68]
 
-    SY.wait_ge(S.v, n_sr)
+    zs = [blk(T.psA, i) for i in range(4)] + [blk(T.psB, i) for i in range(4)]
+    x = [tt(blk(T.psX, 3 + i // 2) if i % 2 else blk(T.sb, i // 2), zs[i], cb, MAX, b2) for i in range(8)]
+    y = [tt(blk(T.psY, i // 2) if i % 2 else blk(T.sb, 4 + i // 2), blk(T.psX, 3 + i), blk(T.sb, i), ADD,
+            [x[2 * i], x[2 * i + 1]]) for i in range(4)]
+    u0 = tt(blk(T.sb, 6), blk(T.psY, 0), blk(T.sb, 4), ADD, [y[0], y[1]])
+    u1 = tt(blk(T.psY, 2), blk(T.psY, 1), blk(T.sb, 5), ADD, [y[2], y[3]])
+    f = tt(blk(T.sb, 7), blk(T.psY, 2), blk(T.sb, 6), ADD, [u0, u1])
+    k = halves(T.sb, 448, 64, ADD, T.tc, T.tot, 0, f)
+    k_sr = tt(T.sr[:], T.tot[:], T.c128[:], SUB, [k, k_c128])
+
+    SY.wait_ge(dsem(k_sr), 1)
     SY.dma_start(T.land2[rank], T.sr[:]).then_inc(S.st2, 16)
     g.wait_ge(S.st2, 16)
     nloc += allgather(T.land2, S.arr2)
@@ -194,10 +192,9 @@ def rank_program(g, core, T, topo):
     PE.wait_ge(S.l2, 16)
     PE.wait_ge(S.sel, 16)
     PE.matmul(T.psS[0:4, 0:128], T.sel[:], T.L2[:], True, True).then_inc(S.t2, 1)
-    sync()
     V.wait_ge(S.t2, 1)
-    n_out = cp(T.srow[:], T.psS[0:4, 0:128])
-    SY.wait_ge(S.v, n_out)
+    k_out = cp(T.srow[:], T.psS[0:4, 0:128], [])
+    SY.wait_ge(dsem(k_out), 1)
     SY.dma_start(T.s[:], T.srow[:]).then_inc(S.sout, 16)
 
     g.wait_ge(S.loc, nloc)

@@ -1,44 +1,38 @@
 from concourse.bass import DstId, RemoteDMATransfer
-from concourse.mybir import AluOpType
+from concourse.mybir import AluOpType, AxisListType, ActivationFunctionType
 
 N, TK = 16, 512
-NOPS = 64
 
 SCRATCH = {
     "h_sb": ("sbuf", [128, 512], "bfloat16"),
     "w_sb": ("sbuf", [128, 128], "bfloat16"),
-    "psA": ("psum", [128, 512], "float32"),
-    "psB": ("psum", [128, 512], "float32"),
-    "psT": ("psum", [128, 512], "float32"),
-    "psX": ("psum", [128, 512], "float32"),
-    "psY": ("psum", [128, 512], "float32"),
-    "psS": ("psum", [128, 512], "float32"),
-    "sa": ("sbuf", [128, 512], "float32"),
-    "sb": ("sbuf", [128, 512], "float32"),
-    "ta": ("sbuf", [128, 128], "float32"),
-    "tb": ("sbuf", [128, 128], "float32"),
-    "tc": ("sbuf", [128, 128], "float32"),
-    "u64": ("sbuf", [128, 64], "float32"),
+    "z0": ("psum", [128, 512], "float32"),
+    "z1": ("psum", [128, 512], "float32"),
+    "z2": ("psum", [128, 512], "float32"),
+    "z3": ("psum", [128, 512], "float32"),
+    "t0": ("psum", [128, 512], "float32"),
+    "t1": ("psum", [128, 512], "float32"),
+    "t2": ("psum", [128, 512], "float32"),
+    "t3": ("psum", [128, 512], "float32"),
     "lm": ("sbuf", [128, 4], "float32"),
-    "mc": ("sbuf", [128, 68], "float32"),
-    "c128": ("sbuf", [128, 4], "float32"),
-    "tot": ("sbuf", [128, 4], "float32"),
+    "negc": ("sbuf", [128, 16], "float32"),
+    "mg": ("sbuf", [128, 4], "float32"),
     "sr": ("sbuf", [128, 4], "float32"),
-    "kc": ("sbuf", [128, 4], "float32"),
-    "pat": ("sbuf", [16, 34], "float32"),
-    "patS": ("sbuf", [16, 16], "float32"),
-    "idr": ("dram", [17, 32], "float32"),
-    "seld": ("dram", [64, 4], "float32"),
+    "relu": ("sbuf", [128, 512], "float32"),
+    "val": ("sbuf", [16, 32], "float32"),
     "eye": ("sbuf", [16, 32], "float32"),
-    "sel": ("sbuf", [64, 4], "float32"),
+    "ones": ("sbuf", [128, 128], "float32"),
+    "idn": ("sbuf", [128, 128], "float32"),
+    "sel": ("sbuf", [128, 8], "float32"),
     "land1": ("dram", [16, 128, 4], "float32"),
     "land2": ("dram", [16, 128, 4], "float32"),
     "L1": ("sbuf", [16, 512], "float32"),
-    "L2": ("sbuf", [64, 128], "float32"),
-    "srow": ("sbuf", [4, 128], "float32"),
+    "L2": ("sbuf", [128, 64], "float32"),
+    "srow": ("sbuf", [8, 64], "float32"),
 }
-SEMAPHORES = ["h", "w", "mma", "mmb", "c1", "c2", "eye", "sel", "st1", "st2", "arr1", "arr2", "loc",
-              "l1", "l2", "t1", "t2", "mout", "sout"] + ["d%d" % i for i in range(NOPS)]
+SEMAPHORES = ["h", "w", "f1", "f2", "eye", "idn", "sel", "red", "st1", "st2", "arr1", "arr2", "loc",
+              "l1", "l2", "mr", "acc", "fin", "cp", "mout", "sout"] + \
+             ["mm%d" % j for j in range(4)] + ["tt%d" % j for j in range(4)] + ["nc%d" % j for j in range(4)]
 
 
 def rank_program(g, core, T, topo):
@@ -47,52 +41,10 @@ def rank_program(g, core, T, topo):
         return
     S = T.sem
     V, PE, SY, SC = g.vector, g.tensor, g.sync, g.scalar
-    MAX, ADD, SUB, MUL = AluOpType.max, AluOpType.add, AluOpType.subtract, AluOpType.mult
-    anc = []
-    seen = set()
-
-    def dsem(k):
-        return S["d%d" % k]
-
-    def need(deps):
-        for d in deps:
-            if d not in seen:
-                V.wait_ge(dsem(d), 1)
-                seen.add(d)
-                seen.update(anc[d])
-
-    def done(ins, deps):
-        k = len(anc)
-        ins.then_inc(dsem(k), 1)
-        a = set(deps)
-        for d in deps:
-            a.update(anc[d])
-        anc.append(a)
-        return k
-
-    def tt(out, a, b, op, deps):
-        need(deps)
-        return done(V.tensor_tensor(out, a, b, op), deps)
-
-    def cp(out, a, deps):
-        need(deps)
-        return done(V.tensor_copy(out, a), deps)
-
-    def fill(ap, val, deps=()):
-        need(deps)
-        return done(V.memset(ap, val), deps)
-
-    def halves(src, base, width, op, lv, last, lbase, dep, stop=4):
-        off = 0
-        while width > stop:
-            width //= 2
-            dst, dbase = (last, lbase) if width == stop else (lv, off)
-            dep = tt(dst[:, dbase:dbase + width], src[:, base:base + width], src[:, base + width:base + 2 * width], op, [dep])
-            src, base, off = dst, dbase, off + width
-        return dep
-
-    def blk(buf, i):
-        return buf[:, 64 * i:64 * i + 64]
+    MAX, ADD, EQ = AluOpType.max, AluOpType.add, AluOpType.is_equal
+    X = AxisListType.X
+    Z = [T.z0, T.z1, T.z2, T.z3]
+    P = [T.t0, T.t1, T.t2, T.t3]
 
     peers = [c for c in T.cores if c != core]
     common = topo.mask(core, peers[0])
@@ -118,71 +70,51 @@ def rank_program(g, core, T, topo):
     SY.dma_start(T.h_sb[:], T.h[:]).then_inc(S.h, 16)
     SC.dma_start(T.w_sb[:], T.w[:]).then_inc(S.w, 16)
 
-    fp = [fill(T.pat[:, 0:1], 1.0), fill(T.pat[:, 1:2], 0.5), fill(T.pat[:, 2:34], 0.0)]
-    f_kc = fill(T.kc[:], 64.0)
-    f0 = fill(T.patS[:], 0.0)
-    fs = [fill(T.patS[:, 5 * k:5 * k + 1], 1.0, [f0]) for k in range(4)]
-    for k in fp + fs:
-        SC.wait_ge(dsem(k), 1)
-    SC.wait_ge(S.h, 16)
-    SC.dma_start(T.idr[:], T.pat[:]).then_inc(S.c1, 16)
-    SC.dma_start(T.seld[:], T.patS[:]).then_inc(S.c2, 16)
-    SC.wait_ge(S.c1, 16)
-    SC.dma_start(T.eye[:], T.idr[0:16, :]).then_inc(S.eye, 16)
-    SC.wait_ge(S.c2, 16)
-    SC.dma_start(T.sel[:], T.seld[:]).then_inc(S.sel, 16)
+    V.memset(T.val[:, 0:16], 1.0).then_inc(S.f1, 1)
+    V.memset(T.val[:, 16:32], 0.5).then_inc(S.f1, 1)
+    V.memset(T.ones[:], 1.0).then_inc(S.f2, 1)
+    g.wait_ge(S.f1, 2)
+    g.affine_select(T.eye[:], T.val[:], [[0, 2], [-1, 16]], EQ, 0.0, 0, 1).then_inc(S.eye, 1)
+    g.wait_ge(S.f2, 1)
+    g.affine_select(T.idn[:], T.ones[:], [[-1, 128]], EQ, 0.0, 0, 1).then_inc(S.idn, 1)
 
     PE.wait_ge(S.h, 16)
     PE.wait_ge(S.w, 16)
     for j in range(4):
-        PE.matmul(T.psA[:, j:256:4], T.h_sb[:, j::4], T.w_sb[:, 0:64], True, True).then_inc(S.mma, 1)
+        PE.matmul(Z[j][:, 0:128], T.h_sb[:, j::4], T.w_sb[:], True, True).then_inc(S["mm%d" % j], 1)
     for j in range(4):
-        PE.matmul(T.psB[:, j:256:4], T.h_sb[:, j::4], T.w_sb[:, 64:128], True, True).then_inc(S.mmb, 1)
+        V.wait_ge(S["mm%d" % j], 1)
+        V.tensor_reduce(T.lm[:, j:j + 1], Z[j][:, 0:128], X, MAX).then_inc(S.red, 1)
 
-    V.wait_ge(S.mma, 4)
-    c = [cp(blk(T.sa, i), blk(T.psA, i), []) for i in range(4)]
-    V.wait_ge(S.mmb, 4)
-    l1 = [tt(blk(T.psX, i // 2) if i % 2 else blk(T.sa, 4 + i // 2), blk(T.psB, i), blk(T.sa, i), MAX, [c[i]])
-          for i in range(4)]
-    l2a = tt(blk(T.sa, 6), blk(T.psX, 0), blk(T.sa, 4), MAX, [l1[0], l1[1]])
-    l2b = tt(blk(T.psX, 2), blk(T.psX, 1), blk(T.sa, 5), MAX, [l1[2], l1[3]])
-    l3 = tt(blk(T.sa, 7), blk(T.psX, 2), blk(T.sa, 6), MAX, [l2a, l2b])
-    k_lm = halves(T.sa, 448, 64, MAX, T.ta, T.lm, 0, l3)
-
-    SY.wait_ge(dsem(k_lm), 1)
+    SY.wait_ge(S.red, 4)
     SY.dma_start(T.land1[rank], T.lm[:]).then_inc(S.st1, 16)
     g.wait_ge(S.st1, 16)
     nloc = allgather(T.land1, S.arr1)
     SY.wait_ge(S.st1, 16)
     SY.wait_ge(S.arr1, len(peers))
     SY.dma_start(T.L1[:], T.land1[:]).then_inc(S.l1, 16)
+
+    V.wait_ge(S.idn, 1)
+    for q in range(8):
+        V.tensor_reduce(T.sel[:, q:q + 1], T.idn[:, q::8], X, ADD).then_inc(S.sel, 1)
+
     PE.wait_ge(S.l1, 16)
-    PE.wait_ge(S.eye, 16)
+    PE.wait_ge(S.eye, 1)
     for j in range(4):
-        PE.matmul(T.psT[:, j:128:4], T.L1[:, j::4], T.eye[:], True, True).then_inc(S.t1, 1)
-    V.wait_ge(S.t1, 4)
-    k = cp(T.u64[:], T.psT[:, 64:128], [])
-    k = tt(T.tb[:, 64:128], T.psT[:, 0:64], T.u64[:], MAX, [k])
-    k_gm = halves(T.tb, 64, 64, MAX, T.tb, T.mc, 0, k, stop=8)
-    SC.wait_ge(dsem(k_gm), 1)
-    SC.dma_start(T.m[:], T.mc[:, 0:4]).then_inc(S.mout, 16)
+        PE.matmul(P[j][:, 0:32], T.L1[:, j::4], T.eye[:], True, True).then_inc(S["tt%d" % j], 1)
+    for j in range(4):
+        V.wait_ge(S["tt%d" % j], 1)
+        V.tensor_reduce(T.negc[:, 4 * j:4 * j + 1], P[j][:, 16:32], X, MAX, negate=True).then_inc(S["nc%d" % j], 1)
+    for j in range(4):
+        V.tensor_reduce(T.mg[:, j:j + 1], P[j][:, 0:16], X, MAX).then_inc(S.mr, 1)
+    for j in range(4):
+        SC.wait_ge(S["nc%d" % j], 1)
+        SC.activation(T.relu[:, 128 * j:128 * j + 128], Z[j][:, 0:128], ActivationFunctionType.Relu,
+                      bias=T.negc[:, 4 * j:4 * j + 1], scale=1.0, accum_out=T.sr[:, j:j + 1]).then_inc(S.acc, 1)
+    SC.wait_ge(S.mr, 4)
+    SC.dma_start(T.m[:], T.mg[:]).then_inc(S.mout, 16)
 
-    b1 = [cp(T.mc[:, 4 + 4 * i:8 + 4 * i], T.mc[:, 4:8], [k_gm]) for i in range(1, 4)]
-    k_c128 = tt(T.c128[:], T.mc[:, 0:4], T.kc[:], MUL, [k_gm, f_kc])
-    b2 = [cp(T.mc[:, 4 + 16 * i:20 + 16 * i], T.mc[:, 4:20], b1) for i in range(1, 4)]
-    cb = T.mc[:, 4:68]
-
-    zs = [blk(T.psA, i) for i in range(4)] + [blk(T.psB, i) for i in range(4)]
-    x = [tt(blk(T.psX, 3 + i // 2) if i % 2 else blk(T.sb, i // 2), zs[i], cb, MAX, b2) for i in range(8)]
-    y = [tt(blk(T.psY, i // 2) if i % 2 else blk(T.sb, 4 + i // 2), blk(T.psX, 3 + i), blk(T.sb, i), ADD,
-            [x[2 * i], x[2 * i + 1]]) for i in range(4)]
-    u0 = tt(blk(T.sb, 6), blk(T.psY, 0), blk(T.sb, 4), ADD, [y[0], y[1]])
-    u1 = tt(blk(T.psY, 2), blk(T.psY, 1), blk(T.sb, 5), ADD, [y[2], y[3]])
-    f = tt(blk(T.sb, 7), blk(T.psY, 2), blk(T.sb, 6), ADD, [u0, u1])
-    k = halves(T.sb, 448, 64, ADD, T.tc, T.tot, 0, f)
-    k_sr = tt(T.sr[:], T.tot[:], T.c128[:], SUB, [k, k_c128])
-
-    SY.wait_ge(dsem(k_sr), 1)
+    SY.wait_ge(S.acc, 4)
     SY.dma_start(T.land2[rank], T.sr[:]).then_inc(S.st2, 16)
     g.wait_ge(S.st2, 16)
     nloc += allgather(T.land2, S.arr2)
@@ -190,11 +122,12 @@ def rank_program(g, core, T, topo):
     SY.wait_ge(S.arr2, len(peers))
     SY.dma_start(T.L2[:], T.land2[:]).then_inc(S.l2, 16)
     PE.wait_ge(S.l2, 16)
-    PE.wait_ge(S.sel, 16)
-    PE.matmul(T.psS[0:4, 0:128], T.sel[:], T.L2[:], True, True).then_inc(S.t2, 1)
-    V.wait_ge(S.t2, 1)
-    k_out = cp(T.srow[:], T.psS[0:4, 0:128], [])
-    SY.wait_ge(dsem(k_out), 1)
+    PE.wait_ge(S.sel, 8)
+    PE.wait_ge(S.mr, 4)
+    PE.matmul(T.t0[0:8, 0:64], T.sel[:], T.L2[:], True, True).then_inc(S.fin, 1)
+    V.wait_ge(S.fin, 1)
+    V.tensor_copy(T.srow[:], T.t0[0:8, 0:64]).then_inc(S.cp, 1)
+    SY.wait_ge(S.cp, 1)
     SY.dma_start(T.s[:], T.srow[:]).then_inc(S.sout, 16)
 
     g.wait_ge(S.loc, nloc)

@@ -2,37 +2,36 @@ from concourse.bass import DstId, RemoteDMATransfer
 from concourse.mybir import AluOpType, AxisListType, ActivationFunctionType
 
 N, TK = 16, 512
+HALF = TK // 2
 
 SCRATCH = {
     "h_sb": ("sbuf", [128, 512], "bfloat16"),
     "w_sb": ("sbuf", [128, 128], "bfloat16"),
-    "z0": ("psum", [128, 512], "float32"),
-    "z1": ("psum", [128, 512], "float32"),
-    "z2": ("psum", [128, 512], "float32"),
-    "z3": ("psum", [128, 512], "float32"),
-    "t0": ("psum", [128, 512], "float32"),
-    "t1": ("psum", [128, 512], "float32"),
-    "t2": ("psum", [128, 512], "float32"),
-    "t3": ("psum", [128, 512], "float32"),
-    "lm": ("sbuf", [128, 4], "float32"),
     "negc": ("sbuf", [128, 16], "float32"),
-    "mg": ("sbuf", [128, 4], "float32"),
-    "sr": ("sbuf", [128, 4], "float32"),
     "relu": ("sbuf", [128, 512], "float32"),
     "val": ("sbuf", [16, 32], "float32"),
     "eye": ("sbuf", [16, 32], "float32"),
     "ones": ("sbuf", [128, 128], "float32"),
     "idn": ("sbuf", [128, 128], "float32"),
     "sel": ("sbuf", [128, 8], "float32"),
-    "land1": ("dram", [16, 128, 4], "float32"),
-    "land2": ("dram", [16, 128, 4], "float32"),
-    "L1": ("sbuf", [16, 512], "float32"),
-    "L2": ("sbuf", [128, 64], "float32"),
-    "srow": ("sbuf", [8, 64], "float32"),
 }
-SEMAPHORES = ["h", "w", "f1", "f2", "eye", "idn", "sel", "red", "st1", "st2", "arr1", "arr2", "loc",
-              "l1", "l2", "mr", "acc", "fin", "cp", "mout", "sout"] + \
-             ["mm%d" % j for j in range(4)] + ["tt%d" % j for j in range(4)] + ["nc%d" % j for j in range(4)]
+for _k in range(4):
+    SCRATCH["z%d" % _k] = ("psum", [128, 512], "float32")
+    SCRATCH["t%d" % _k] = ("psum", [128, 512], "float32")
+for _H in range(2):
+    SCRATCH["lm%d" % _H] = ("sbuf", [128, 4], "float32")
+    SCRATCH["mg%d" % _H] = ("sbuf", [128, 4], "float32")
+    SCRATCH["sr%d" % _H] = ("sbuf", [128, 4], "float32")
+    SCRATCH["landm%d" % _H] = ("dram", [16, 128, 2], "float32")
+    SCRATCH["lands%d" % _H] = ("dram", [16, 128, 2], "float32")
+    SCRATCH["Lm%d" % _H] = ("sbuf", [16, 256], "float32")
+    SCRATCH["Ls%d" % _H] = ("sbuf", [128, 32], "float32")
+    SCRATCH["srow%d" % _H] = ("sbuf", [8, 32], "float32")
+
+SEMAPHORES = ["w", "f1", "f2", "eye", "idn", "sel", "loc"] + \
+             [n + str(H) for H in range(2) for n in ("h", "red", "st1_", "st2_", "arr1_", "arr2_", "l1_", "l2_", "mr",
+                                                     "acc", "fin", "cp", "mout", "sout")] + \
+             [n + str(k) for k in range(4) for n in ("mm", "tt", "nc")]
 
 
 def rank_program(g, core, T, topo):
@@ -45,6 +44,10 @@ def rank_program(g, core, T, topo):
     X = AxisListType.X
     Z = [T.z0, T.z1, T.z2, T.z3]
     P = [T.t0, T.t1, T.t2, T.t3]
+    HS = (0, 1)
+
+    def sem(name, i):
+        return S[name + str(i)]
 
     peers = [c for c in T.cores if c != core]
     common = topo.mask(core, peers[0])
@@ -52,7 +55,7 @@ def rank_program(g, core, T, topo):
         common &= topo.mask(core, d)
     engines = [1 << b for b in range(16) if (common >> b) & 1]
 
-    def allgather(buf, sem):
+    def allgather(buf, arrived):
         trs = []
         for e, eng in enumerate(engines):
             mine = peers[e::len(engines)]
@@ -62,13 +65,14 @@ def rank_program(g, core, T, topo):
             for d in mine:
                 rid, pid = topo.addr(d, core)
                 ids.append(DstId(rid=rid, pnc=pid))
-            trs.append(RemoteDMATransfer(dst_ids=ids, dma_engine_mask=eng, remote_sem=sem,
+            trs.append(RemoteDMATransfer(dst_ids=ids, dma_engine_mask=eng, remote_sem=arrived,
                                          srcs=[buf[rank]], dsts=[buf[rank] for _ in mine]))
         g.remote_dma_fused(trs, local_sem=S.loc)
         return len(trs)
 
-    SY.dma_start(T.h_sb[:], T.h[:]).then_inc(S.h, 16)
     SC.dma_start(T.w_sb[:], T.w[:]).then_inc(S.w, 16)
+    for H in HS:
+        SY.dma_start(T.h_sb[:, HALF * H:HALF * H + HALF], T.h[:, HALF * H:HALF * H + HALF]).then_inc(sem("h", H), 16)
 
     V.memset(T.val[:, 0:16], 1.0).then_inc(S.f1, 1)
     V.memset(T.val[:, 16:32], 0.5).then_inc(S.f1, 1)
@@ -78,58 +82,85 @@ def rank_program(g, core, T, topo):
     g.wait_ge(S.f2, 1)
     g.affine_select(T.idn[:], T.ones[:], [[-1, 128]], EQ, 0.0, 0, 1).then_inc(S.idn, 1)
 
-    PE.wait_ge(S.h, 16)
     PE.wait_ge(S.w, 16)
-    for j in range(4):
-        PE.matmul(Z[j][:, 0:128], T.h_sb[:, j::4], T.w_sb[:], True, True).then_inc(S["mm%d" % j], 1)
-    for j in range(4):
-        V.wait_ge(S["mm%d" % j], 1)
-        V.tensor_reduce(T.lm[:, j:j + 1], Z[j][:, 0:128], X, MAX).then_inc(S.red, 1)
+    for H in HS:
+        PE.wait_ge(sem("h", H), 16)
+        for j in range(2):
+            k = 2 * H + j
+            PE.matmul(Z[k][:, 0:128], T.h_sb[:, HALF * H + j:HALF * H + HALF:2], T.w_sb[:], True, True) \
+                .then_inc(sem("mm", k), 1)
+    for H in HS:
+        for j in range(2):
+            k = 2 * H + j
+            V.wait_ge(sem("mm", k), 1)
+            V.tensor_reduce(T["lm%d" % H][:, j:j + 1], Z[k][:, 0:128], X, MAX).then_inc(sem("red", H), 1)
 
-    SY.wait_ge(S.red, 4)
-    SY.dma_start(T.land1[rank], T.lm[:]).then_inc(S.st1, 16)
-    g.wait_ge(S.st1, 16)
-    nloc = allgather(T.land1, S.arr1)
-    SY.wait_ge(S.st1, 16)
-    SY.wait_ge(S.arr1, len(peers))
-    SY.dma_start(T.L1[:], T.land1[:]).then_inc(S.l1, 16)
+    nloc = 0
+    for H in HS:
+        SY.wait_ge(sem("red", H), 2)
+        SY.dma_start(T["landm%d" % H][rank], T["lm%d" % H][:, 0:2]).then_inc(sem("st1_", H), 16)
+        g.wait_ge(sem("st1_", H), 16)
+        nloc += allgather(T["landm%d" % H], sem("arr1_", H))
+    for H in HS:
+        SY.wait_ge(sem("st1_", H), 16)
+        SY.wait_ge(sem("arr1_", H), len(peers))
+        SY.dma_start(T["Lm%d" % H][:], T["landm%d" % H][:]).then_inc(sem("l1_", H), 16)
 
     V.wait_ge(S.idn, 1)
     for q in range(8):
         V.tensor_reduce(T.sel[:, q:q + 1], T.idn[:, q::8], X, ADD).then_inc(S.sel, 1)
 
-    PE.wait_ge(S.l1, 16)
     PE.wait_ge(S.eye, 1)
-    for j in range(4):
-        PE.matmul(P[j][:, 0:32], T.L1[:, j::4], T.eye[:], True, True).then_inc(S["tt%d" % j], 1)
-    for j in range(4):
-        V.wait_ge(S["tt%d" % j], 1)
-        V.tensor_reduce(T.negc[:, 4 * j:4 * j + 1], P[j][:, 16:32], X, MAX, negate=True).then_inc(S["nc%d" % j], 1)
-    for j in range(4):
-        V.tensor_reduce(T.mg[:, j:j + 1], P[j][:, 0:16], X, MAX).then_inc(S.mr, 1)
-    for j in range(4):
-        SC.wait_ge(S["nc%d" % j], 1)
-        SC.activation(T.relu[:, 128 * j:128 * j + 128], Z[j][:, 0:128], ActivationFunctionType.Relu,
-                      bias=T.negc[:, 4 * j:4 * j + 1], scale=1.0, accum_out=T.sr[:, j:j + 1]).then_inc(S.acc, 1)
-    SC.wait_ge(S.mr, 4)
-    SC.dma_start(T.m[:], T.mg[:]).then_inc(S.mout, 16)
+    for H in HS:
+        PE.wait_ge(sem("l1_", H), 16)
+        for j in range(2):
+            k = 2 * H + j
+            PE.matmul(P[k][:, 0:32], T["Lm%d" % H][:, j::2], T.eye[:], True, True).then_inc(sem("tt", k), 1)
+    for H in HS:
+        for j in range(2):
+            k = 2 * H + j
+            V.wait_ge(sem("tt", k), 1)
+            V.tensor_reduce(T.negc[:, 4 * k:4 * k + 1], P[k][:, 16:32], X, MAX, negate=True).then_inc(sem("nc", k), 1)
+        for j in range(2):
+            k = 2 * H + j
+            V.tensor_reduce(T["mg%d" % H][:, j:j + 1], P[k][:, 0:16], X, MAX).then_inc(sem("mr", H), 1)
+    for H in HS:
+        for j in range(2):
+            k = 2 * H + j
+            SC.wait_ge(sem("nc", k), 1)
+            SC.activation(T.relu[:, 128 * k:128 * k + 128], Z[k][:, 0:128], ActivationFunctionType.Relu,
+                          bias=T.negc[:, 4 * k:4 * k + 1], scale=1.0,
+                          accum_out=T["sr%d" % H][:, j:j + 1]).then_inc(sem("acc", H), 1)
 
-    SY.wait_ge(S.acc, 4)
-    SY.dma_start(T.land2[rank], T.sr[:]).then_inc(S.st2, 16)
-    g.wait_ge(S.st2, 16)
-    nloc += allgather(T.land2, S.arr2)
-    SY.wait_ge(S.st2, 16)
-    SY.wait_ge(S.arr2, len(peers))
-    SY.dma_start(T.L2[:], T.land2[:]).then_inc(S.l2, 16)
-    PE.wait_ge(S.l2, 16)
+    for H in HS:
+        SY.wait_ge(sem("acc", H), 2)
+        SY.dma_start(T["lands%d" % H][rank], T["sr%d" % H][:, 0:2]).then_inc(sem("st2_", H), 16)
+        g.wait_ge(sem("st2_", H), 16)
+        nloc += allgather(T["lands%d" % H], sem("arr2_", H))
+
+    SC.wait_ge(sem("st2_", 1), 16)
+    for H in HS:
+        SC.wait_ge(sem("mr", H), 2)
+        SC.dma_start(T.m[:, HALF * H:HALF * H + HALF], T["mg%d" % H][:, 0:2]).then_inc(sem("mout", H), 16)
+
+    for H in HS:
+        SY.wait_ge(sem("st2_", H), 16)
+        SY.wait_ge(sem("arr2_", H), len(peers))
+        SY.dma_start(T["Ls%d" % H][:], T["lands%d" % H][:]).then_inc(sem("l2_", H), 16)
     PE.wait_ge(S.sel, 8)
-    PE.wait_ge(S.mr, 4)
-    PE.matmul(T.t0[0:8, 0:64], T.sel[:], T.L2[:], True, True).then_inc(S.fin, 1)
-    V.wait_ge(S.fin, 1)
-    V.tensor_copy(T.srow[:], T.t0[0:8, 0:64]).then_inc(S.cp, 1)
-    SY.wait_ge(S.cp, 1)
-    SY.dma_start(T.s[:], T.srow[:]).then_inc(S.sout, 16)
+    for H in HS:
+        PE.wait_ge(sem("l2_", H), 16)
+        PE.wait_ge(sem("nc", 2 * H), 1)
+        PE.wait_ge(sem("mr", H), 2)
+        PE.matmul(P[2 * H][0:8, 0:32], T.sel[:], T["Ls%d" % H][:], True, True).then_inc(sem("fin", H), 1)
+    for H in HS:
+        V.wait_ge(sem("fin", H), 1)
+        V.tensor_copy(T["srow%d" % H][:], P[2 * H][0:8, 0:32]).then_inc(sem("cp", H), 1)
+    for H in HS:
+        SY.wait_ge(sem("cp", H), 1)
+        SY.dma_start(T.s[:, HALF * H:HALF * H + HALF], T["srow%d" % H][:]).then_inc(sem("sout", H), 16)
 
     g.wait_ge(S.loc, nloc)
-    SC.wait_ge(S.mout, 16)
-    SY.wait_ge(S.sout, 16)
+    for H in HS:
+        SC.wait_ge(sem("mout", H), 16)
+        SY.wait_ge(sem("sout", H), 16)

@@ -55,10 +55,10 @@ def rank_program(g, core, T, topo):
         common &= topo.mask(core, d)
     engines = [1 << b for b in range(16) if (common >> b) & 1]
 
-    def allgather(buf, arrived):
+    def allgather(buf, arrived, dests):
         trs = []
         for e, eng in enumerate(engines):
-            mine = peers[e::len(engines)]
+            mine = dests[e::len(engines)]
             if not mine:
                 continue
             ids = []
@@ -96,14 +96,27 @@ def rank_program(g, core, T, topo):
             V.tensor_reduce(T["lm%d" % H][:, j:j + 1], Z[k][:, 0:128], X, MAX).then_inc(sem("red", H), 1)
 
     nloc = 0
+    nxt = T.cores[(rank + 1) % N]
+    nwide = 1
+    while 2 * nwide <= len(engines):
+        nwide *= 2
+    wide = 0
+    for eng in engines[:nwide]:
+        wide |= eng
+    rid, pid = topo.addr(nxt, core)
+    g.wait_ge(sem("red", 0), 2)
+    g.remote_dma(T.landm0[rank], T.lm0[:, 0:2], sem("arr1_", 0), S.loc, pid, rid, wide)
+    nloc += nwide
+    dests1 = ([c for c in peers if c != nxt], peers)
+    need1 = (len(peers) - 1 + nwide, len(peers))
     for H in HS:
         SY.wait_ge(sem("red", H), 2)
         SY.dma_start(T["landm%d" % H][rank], T["lm%d" % H][:, 0:2]).then_inc(sem("st1_", H), 16)
         g.wait_ge(sem("st1_", H), 16)
-        nloc += allgather(T["landm%d" % H], sem("arr1_", H))
+        nloc += allgather(T["landm%d" % H], sem("arr1_", H), dests1[H])
     for H in HS:
         SY.wait_ge(sem("st1_", H), 16)
-        SY.wait_ge(sem("arr1_", H), len(peers))
+        SY.wait_ge(sem("arr1_", H), need1[H])
         SY.dma_start(T["Lm%d" % H][:], T["landm%d" % H][:]).then_inc(sem("l1_", H), 16)
 
     V.wait_ge(S.idn, 1)
@@ -121,6 +134,7 @@ def rank_program(g, core, T, topo):
             k = 2 * H + j
             V.wait_ge(sem("tt", k), 1)
             V.tensor_reduce(T.negc[:, 4 * k:4 * k + 1], P[k][:, 16:32], X, MAX, negate=True).then_inc(sem("nc", k), 1)
+    for H in HS:
         for j in range(2):
             k = 2 * H + j
             V.tensor_reduce(T["mg%d" % H][:, j:j + 1], P[k][:, 0:16], X, MAX).then_inc(sem("mr", H), 1)
@@ -136,7 +150,7 @@ def rank_program(g, core, T, topo):
         SY.wait_ge(sem("acc", H), 2)
         SY.dma_start(T["lands%d" % H][rank], T["sr%d" % H][:, 0:2]).then_inc(sem("st2_", H), 16)
         g.wait_ge(sem("st2_", H), 16)
-        nloc += allgather(T["lands%d" % H], sem("arr2_", H))
+        nloc += allgather(T["lands%d" % H], sem("arr2_", H), peers)
 
     SC.wait_ge(sem("st2_", 1), 16)
     for H in HS:

from concourse.bass import DstId, RemoteDMATransfer
from concourse.mybir import AluOpType, AxisListType, ActivationFunctionType

N, TK = 16, 512
HALF = TK // 2

SCRATCH = {
    "h_sb": ("sbuf", [128, 512], "bfloat16"),
    "w_sb": ("sbuf", [128, 128], "bfloat16"),
    "negc": ("sbuf", [128, 16], "float32"),
    "relu": ("sbuf", [128, 512], "float32"),
    "val": ("sbuf", [16, 32], "float32"),
    "eye": ("sbuf", [16, 32], "float32"),
    "ones": ("sbuf", [128, 128], "float32"),
    "idn": ("sbuf", [128, 128], "float32"),
    "sel": ("sbuf", [128, 8], "float32"),
}
for _k in range(4):
    SCRATCH["z%d" % _k] = ("psum", [128, 512], "float32")
    SCRATCH["t%d" % _k] = ("psum", [128, 512], "float32")
for _H in range(2):
    SCRATCH["lm%d" % _H] = ("sbuf", [128, 4], "float32")
    SCRATCH["mg%d" % _H] = ("sbuf", [128, 4], "float32")
    SCRATCH["sr%d" % _H] = ("sbuf", [128, 4], "float32")
    SCRATCH["landm%d" % _H] = ("dram", [16, 128, 2], "float32")
    SCRATCH["lands%d" % _H] = ("dram", [16, 128, 2], "float32")
    SCRATCH["Lm%d" % _H] = ("sbuf", [16, 256], "float32")
    SCRATCH["Ls%d" % _H] = ("sbuf", [128, 32], "float32")
    SCRATCH["srow%d" % _H] = ("sbuf", [8, 32], "float32")

SEMAPHORES = ["w", "f1", "f2", "eye", "idn", "sel", "loc"] + \
             [n + str(H) for H in range(2) for n in ("h", "red", "st1_", "st2_", "arr1_", "arr2_", "l1_", "l2_", "mr",
                                                     "acc", "fin", "cp", "mout", "sout")] + \
             [n + str(k) for k in range(4) for n in ("mm", "tt", "nc")]


def rank_program(g, core, T, topo):
    rank = T.rank_of(core)
    if rank is None:
        return
    S = T.sem
    V, PE, SY, SC = g.vector, g.tensor, g.sync, g.scalar
    MAX, ADD, EQ = AluOpType.max, AluOpType.add, AluOpType.is_equal
    X = AxisListType.X
    Z = [T.z0, T.z1, T.z2, T.z3]
    P = [T.t0, T.t1, T.t2, T.t3]
    HS = (0, 1)

    def sem(name, i):
        return S[name + str(i)]

    peers = [c for c in T.cores if c != core]
    common = topo.mask(core, peers[0])
    for d in peers:
        common &= topo.mask(core, d)
    engines = [1 << b for b in range(16) if (common >> b) & 1]

    def allgather(buf, arrived, dests):
        trs = []
        for e, eng in enumerate(engines):
            mine = dests[e::len(engines)]
            if not mine:
                continue
            ids = []
            for d in mine:
                rid, pid = topo.addr(d, core)
                ids.append(DstId(rid=rid, pnc=pid))
            trs.append(RemoteDMATransfer(dst_ids=ids, dma_engine_mask=eng, remote_sem=arrived,
                                         srcs=[buf[rank]], dsts=[buf[rank] for _ in mine]))
        g.remote_dma_fused(trs, local_sem=S.loc)
        return len(trs)

    SC.dma_start(T.w_sb[:], T.w[:]).then_inc(S.w, 16)
    for H in HS:
        SY.dma_start(T.h_sb[:, HALF * H:HALF * H + HALF], T.h[:, HALF * H:HALF * H + HALF]).then_inc(sem("h", H), 16)

    V.memset(T.val[:, 0:16], 1.0).then_inc(S.f1, 1)
    V.memset(T.val[:, 16:32], 0.5).then_inc(S.f1, 1)
    V.memset(T.ones[:], 1.0).then_inc(S.f2, 1)
    g.wait_ge(S.f1, 2)
    g.affine_select(T.eye[:], T.val[:], [[0, 2], [-1, 16]], EQ, 0.0, 0, 1).then_inc(S.eye, 1)
    g.wait_ge(S.f2, 1)
    g.affine_select(T.idn[:], T.ones[:], [[-1, 128]], EQ, 0.0, 0, 1).then_inc(S.idn, 1)

    PE.wait_ge(S.w, 16)
    for H in HS:
        PE.wait_ge(sem("h", H), 16)
        for j in range(2):
            k = 2 * H + j
            PE.matmul(Z[k][:, 0:128], T.h_sb[:, HALF * H + j:HALF * H + HALF:2], T.w_sb[:], True, True) \
                .then_inc(sem("mm", k), 1)
    for H in HS:
        for j in range(2):
            k = 2 * H + j
            V.wait_ge(sem("mm", k), 1)
            V.tensor_reduce(T["lm%d" % H][:, j:j + 1], Z[k][:, 0:128], X, MAX).then_inc(sem("red", H), 1)

    nloc = 0
    nxt = T.cores[(rank + 1) % N]
    nwide = 1
    while 2 * nwide <= len(engines):
        nwide *= 2
    wide = 0
    for eng in engines[:nwide]:
        wide |= eng
    rid, pid = topo.addr(nxt, core)
    g.wait_ge(sem("red", 0), 2)
    g.remote_dma(T.landm0[rank], T.lm0[:, 0:2], sem("arr1_", 0), S.loc, pid, rid, wide)
    nloc += nwide
    dests1 = ([c for c in peers if c != nxt], peers)
    need1 = (len(peers) - 1 + nwide, len(peers))
    for H in HS:
        SY.wait_ge(sem("red", H), 2)
        SY.dma_start(T["landm%d" % H][rank], T["lm%d" % H][:, 0:2]).then_inc(sem("st1_", H), 16)
        g.wait_ge(sem("st1_", H), 16)
        nloc += allgather(T["landm%d" % H], sem("arr1_", H), dests1[H])
    for H in HS:
        SY.wait_ge(sem("st1_", H), 16)
        SY.wait_ge(sem("arr1_", H), need1[H])
        SY.dma_start(T["Lm%d" % H][:], T["landm%d" % H][:]).then_inc(sem("l1_", H), 16)

    V.wait_ge(S.idn, 1)
    for q in range(8):
        V.tensor_reduce(T.sel[:, q:q + 1], T.idn[:, q::8], X, ADD).then_inc(S.sel, 1)

    PE.wait_ge(S.eye, 1)
    for H in HS:
        PE.wait_ge(sem("l1_", H), 16)
        for j in range(2):
            k = 2 * H + j
            PE.matmul(P[k][:, 0:32], T["Lm%d" % H][:, j::2], T.eye[:], True, True).then_inc(sem("tt", k), 1)
    for H in HS:
        for j in range(2):
            k = 2 * H + j
            V.wait_ge(sem("tt", k), 1)
            V.tensor_reduce(T.negc[:, 4 * k:4 * k + 1], P[k][:, 16:32], X, MAX, negate=True).then_inc(sem("nc", k), 1)
    for H in HS:
        for j in range(2):
            k = 2 * H + j
            V.tensor_reduce(T["mg%d" % H][:, j:j + 1], P[k][:, 0:16], X, MAX).then_inc(sem("mr", H), 1)
    for H in HS:
        for j in range(2):
            k = 2 * H + j
            SC.wait_ge(sem("nc", k), 1)
            SC.activation(T.relu[:, 128 * k:128 * k + 128], Z[k][:, 0:128], ActivationFunctionType.Relu,
                          bias=T.negc[:, 4 * k:4 * k + 1], scale=1.0,
                          accum_out=T["sr%d" % H][:, j:j + 1]).then_inc(sem("acc", H), 1)

    for H in HS:
        SY.wait_ge(sem("acc", H), 2)
        SY.dma_start(T["lands%d" % H][rank], T["sr%d" % H][:, 0:2]).then_inc(sem("st2_", H), 16)
        g.wait_ge(sem("st2_", H), 16)
        nloc += allgather(T["lands%d" % H], sem("arr2_", H), peers)

    SC.wait_ge(sem("st2_", 1), 16)
    for H in HS:
        SC.wait_ge(sem("mr", H), 2)
        SC.dma_start(T.m[:, HALF * H:HALF * H + HALF], T["mg%d" % H][:, 0:2]).then_inc(sem("mout", H), 16)

    for H in HS:
        SY.wait_ge(sem("st2_", H), 16)
        SY.wait_ge(sem("arr2_", H), len(peers))
        SY.dma_start(T["Ls%d" % H][:], T["lands%d" % H][:]).then_inc(sem("l2_", H), 16)
    PE.wait_ge(S.sel, 8)
    for H in HS:
        PE.wait_ge(sem("l2_", H), 16)
        PE.wait_ge(sem("nc", 2 * H), 1)
        PE.wait_ge(sem("mr", H), 2)
        PE.matmul(P[2 * H][0:8, 0:32], T.sel[:], T["Ls%d" % H][:], True, True).then_inc(sem("fin", H), 1)
    for H in HS:
        V.wait_ge(sem("fin", H), 1)
        V.tensor_copy(T["srow%d" % H][:], P[2 * H][0:8, 0:32]).then_inc(sem("cp", H), 1)
    for H in HS:
        SY.wait_ge(sem("cp", H), 1)
        SY.dma_start(T.s[:, HALF * H:HALF * H + HALF], T["srow%d" % H][:]).then_inc(sem("sout", H), 16)

    g.wait_ge(S.loc, nloc)
    for H in HS:
        SC.wait_ge(sem("mout", H), 16)
        SY.wait_ge(sem("sout", H), 16)
